import numpy as np, ml_dtypes
CORES = [88,96,104,112,120,216,224,232,240,248]
N = 10
import mx_ref
NC, WT = 256, 1
BF = ml_dtypes.bfloat16
def setup_inputs(rng):
    def f(*shape):
        return mx_ref.flush((rng.standard_normal(shape, dtype=np.float32) * np.exp2(rng.integers(-2, 3, shape[:-1] + (1,)))).astype(BF))
    return {"w": f(N, 128, WT * 512), "x": f(N, 128, 4 * NC)}
def setup_inputs_blocks(rng):
    d = setup_inputs(rng)
    for k in ("w", "x"): d[k] = mx_ref.spread(d[k], rng, 4)
    return d
def setup_inputs_wide(rng):
    d = setup_inputs(rng)
    for k in ("w", "x"): d[k] = mx_ref.flush((d[k].astype(np.float32) * np.exp2(rng.integers(-8, 9, (N, 1, 1))).astype(np.float32)).astype(BF))
    return d
def setup_inputs_zeros(rng):
    d = setup_inputs(rng); v = d["x"].reshape(N, 128, -1, 4).copy()
    v[np.broadcast_to((rng.random((N, 1, v.shape[2], 1)) < 0.33), v.shape)] = 0
    d["x"] = v.reshape(d["x"].shape)
    return d
def reference(w, x):
    QW = [mx_ref.quantize(w[b // WT][:, 512 * (b % WT):512 * (b % WT) + 512]) for b in range(N * WT)]
    y = np.zeros((N, 128, N * WT * NC), np.float32)
    for r in range(N):
        qx = mx_ref.quantize(x[r])
        for b in range(N * WT):
            y[r][:, NC * b:NC * b + NC] = mx_ref.matmul(QW[b], qx)
    return {"y": y}

from concourse.bass import DstId, RemoteDMATransfer
from concourse.mybir import dt, ActivationFunctionType

N = 10
WC = 128
XC = 256
NSIM = 256
BANK = 512
NBANK = 8
DIRECT = 3
FAN = 2

SCRATCH = {
    "wb": ("sbuf", [128, 4 * WC], "bfloat16"),
    "xb": ("sbuf", [128, 4 * XC], "bfloat16"),
    "xq": ("sbuf", [128, XC], "float8_e4m3fn_x4"),
    "xs": ("sbuf", [128, XC], "uint8"),
    "wq": ("sbuf", [128, N * WC], "float8_e4m3fn_x4"),
    "ws": ("sbuf", [128, N * WC], "uint8"),
    "ps": ("psum", [128, NBANK * BANK], "float32"),
    "yb": ("sbuf", [128, N * XC], "float32"),
}
SEMAPHORES = (["lw", "lx", "qw", "qx", "hs", "hc", "sent", "sta", "stb"]
              + ["arr%d" % j for j in range(N)] + ["mm%d" % j for j in range(N)] + ["cp%d" % j for j in range(N)])

_CACHE = {}


def _place(topo, c):
    return (topo.host(c), topo.chip(c))


def _count(mask):
    return bin(mask).count("1")


def _common_mask(topo, core, dsts):
    m = topo.mask(core, dsts[0])
    for d in dsts[1:]:
        m &= topo.mask(core, d)
    return m


def route_plan(ranks, topo):
    if "plan" in _CACHE:
        return _CACHE["plan"]
    plan = {}
    for s in ranks:
        plane = [d for d in ranks if d == s or topo.same_plane(s, d)]
        i = plane.index(s)
        same = plane[i + 1:] + plane[:i]
        cross = [d for d in ranks if d not in plane]
        cross.sort(key=lambda d: (topo.host(d) != topo.host(s), topo.mates(s, d), d))
        rest = cross + same[DIRECT:]
        groups = [rest[k:k + FAN] for k in range(0, len(rest), FAN)]
        free = [c for c in range(NSIM) if c != s and _place(topo, c) == _place(topo, s)]
        relays = []
        for gi, grp in enumerate(groups):
            fit = [c for c in free
                   if (topo.die(c) == topo.die(s)) == (gi == 0) and all(topo.may_write(c, d) for d in grp)]
            fit.sort(key=lambda c: (sum(1 for d in ranks if topo.may_write(c, d)), c))
            free.remove(fit[0])
            relays.append((fit[0], grp, _common_mask(topo, fit[0], grp)))
        away = _common_mask(topo, s, same[:DIRECT])
        home = _common_mask(topo, s, [h for h, _, _ in relays]) & ~away
        plan[s] = {"direct": same[:DIRECT], "away": away, "relays": relays, "home": home}
    _CACHE["plan"] = plan
    return plan


def _send(g, T, topo, core, j, dsts, mask, sems, after=None):
    ids = []
    for d in dsts:
        rid, pid = topo.addr(d, core)
        ids.append(DstId(rid=rid, pnc=pid))
    a, b = j * WC, (j + 1) * WC
    for p, ap in enumerate((T.ws[:, a:b], T.wq[:, a:b].bitcast(dt.uint8))):
        if after is not None:
            g.wait_ge(after[0][p], after[1])
        g.remote_dma_fused([RemoteDMATransfer(dst_ids=ids, dma_engine_mask=mask, remote_sem=sems[p],
                                              srcs=[ap], dsts=[ap for _ in dsts])], local_sem=T.sem.sent)
    return 2 * _count(mask)


def rank_program(g, core, T, topo):
    ranks = list(T.cores)
    plan = route_plan(ranks, topo)
    rank = T.rank_of(core)

    if rank is None:
        for j, s in enumerate(ranks):
            for h, grp, mask in plan[s]["relays"]:
                if h == core:
                    arr = T.sem["arr%d" % j]
                    left = _send(g, T, topo, core, j, grp, mask, (arr, arr),
                                 after=((T.sem.hs, T.sem.hc), _count(plan[s]["home"])))
                    g.wait_ge(T.sem.sent, left)
        return

    mine = plan[core]
    a, b = rank * WC, (rank + 1) * WC

    g.sync.dma_start(T.wb[:], T.w[:]).then_inc(T.sem.lw, 16)
    g.sync.dma_start(T.xb[:], T.x[:]).then_inc(T.sem.lx, 16)

    g.vector.wait_ge(T.sem.lw, 16)
    g.vector.quantize_mx(T.wq[:, a:b], T.ws[:, a:b], T.wb[:]).then_inc(T.sem.qw, 1)
    g.vector.wait_ge(T.sem.lx, 16)
    g.vector.quantize_mx(T.xq[:], T.xs[:], T.xb[:]).then_inc(T.sem.qx, 1)

    arr = T.sem["arr%d" % rank]
    g.wait_ge(T.sem.qw, 1)
    left = _send(g, T, topo, core, rank, [h for h, _, _ in mine["relays"]], mine["home"], (T.sem.hs, T.sem.hc))
    left += _send(g, T, topo, core, rank, mine["direct"], mine["away"], (arr, arr))

    order = [((0,), rank, 0)]
    for j, s in enumerate(ranks):
        if core in plan[s]["direct"]:
            order.append(((1, plan[s]["direct"].index(core), j), j, 2 * _count(plan[s]["away"])))
        for gi, (h, grp, mask) in enumerate(plan[s]["relays"]):
            if core in grp:
                order.append(((2, grp.index(core), gi, j), j, 2 * _count(mask)))
    order.sort()

    g.tensor.wait_ge(T.sem.qw, 1)
    g.tensor.wait_ge(T.sem.qx, 1)
    stores = [0, 0]
    for k, (_, j, need) in enumerate(order):
        bank = T.ps[:, (k % NBANK) * BANK:(k % NBANK) * BANK + XC]
        mm, cp = T.sem["mm%d" % k], T.sem["cp%d" % k]
        if need:
            g.tensor.wait_ge(T.sem["arr%d" % j], need)
        if k >= NBANK:
            g.tensor.wait_ge(T.sem["cp%d" % (k - NBANK)], 1)
        g.tensor.matmul_mx(bank, T.wq[:, j * WC:(j + 1) * WC], T.ws[:, j * WC:(j + 1) * WC],
                           T.xq[:], T.xs[:], True, True).then_inc(mm, 1)
        yb, y = T.yb[:, j * XC:(j + 1) * XC], T.y[:, j * XC:(j + 1) * XC]
        if k % 2 == 0:
            g.vector.wait_ge(mm, 1)
            g.vector.tensor_copy(yb, bank).then_inc(cp, 1)
            g.sync.wait_ge(cp, 1)
            g.sync.dma_start(y, yb).then_inc(T.sem.sta, 16)
        else:
            g.scalar.wait_ge(mm, 1)
            g.scalar.activation(yb, bank, ActivationFunctionType.Copy).then_inc(cp, 1)
            g.scalar.wait_ge(cp, 1)
            g.scalar.dma_start(y, yb).then_inc(T.sem.stb, 16)
        stores[k % 2] += 16

    g.wait_ge(T.sem.sent, left)
    g.sync.wait_ge(T.sem.sta, stores[0])
    g.scalar.wait_ge(T.sem.stb, stores[1])
